import numpy as np
import ml_dtypes


def mxq(x, axis, fmt="e4m3"):
    dtype, down = {"e4m3": (ml_dtypes.float8_e4m3fn, 7), "e5m2": (ml_dtypes.float8_e5m2, 14)}[fmt]
    v = np.moveaxis(np.asarray(x, np.float32).astype(ml_dtypes.bfloat16).astype(np.float64), axis, -1)
    blocks = v.reshape(v.shape[:-1] + (-1, 32))
    amax = np.abs(blocks).max(-1, keepdims=True)
    byte = np.maximum(np.where(amax > 0, np.frexp(amax)[1] - 1 + 127, 0) - down, 1)
    scale = np.exp2(byte - 127.0)
    codes = (blocks / scale).astype(np.float32).astype(dtype).astype(np.float64)
    return np.moveaxis((codes * scale).reshape(v.shape), -1, axis)


WIDE = False


def mx_kscale(k):
    if not WIDE:
        return np.ones(k)
    levels = np.array([10, -10, 5, -5, 0])
    if k % 512:
        return np.exp2(np.random.permutation(np.resize(levels, k // 32))).repeat(32)
    a = np.empty((k // 512, 16))
    for p in range(k // 512):
        a[p, :8] = np.random.permutation(np.resize(levels, 8))
        for g in range(8):
            far = levels[np.abs(levels - a[p, g]) >= 10]
            a[p, g + 8] = far[np.random.randint(len(far))]
    return np.exp2(a.ravel()).repeat(32)


def f64(x):
    return np.asarray(x).astype(np.float64)


def striped(idx):
    return np.tile(idx.reshape(-1, 16).T, (8, 1)).astype(np.uint16)


def unstriped(offs):
    return offs[:16].T.reshape(-1).astype(np.int64)


E2M1 = np.array([0.0, 0.5, 1.0, 1.5, 2.0, 3.0, 4.0, 6.0, -0.0, -0.5, -1.0, -1.5, -2.0, -3.0, -4.0, -6.0])


def pack_weight(w, fmt):
    k, n = w.shape
    w = f64(np.asarray(w, np.float32).astype(ml_dtypes.bfloat16)).reshape(k // 32, 32, n)
    amax = np.abs(w).max(1)
    if fmt == "e4m3":
        byte = np.frexp(amax)[1] - 1 + 127 - 7
    else:
        mant, ex = np.frexp(amax / 6.0)
        byte = np.where(mant > 0.5, ex, ex - 1) + 127
    byte = np.clip(np.where(amax > 0, byte, 1), 1, 254)
    scaled = (w * np.exp2(127.0 - byte)[:, None, :]).reshape(k, n).astype(np.float32)
    by_word = np.ascontiguousarray(scaled.reshape(k // 512, 128, 4, n).transpose(0, 1, 3, 2))
    if fmt == "e4m3":
        words = by_word.astype(ml_dtypes.float8_e4m3fn).view(np.uint8)
    else:
        c = by_word.astype(ml_dtypes.float4_e2m1fn).view(np.uint8) & 0xF
        words = (c[..., 0::2] | (c[..., 1::2] << 4)).reshape(k // 512, 128, 2 * n)
    return np.ascontiguousarray(words), np.ascontiguousarray(byte.astype(np.uint8).reshape(k // 512, 16, n))


def unpack_weight(words, scales, fmt):
    g, _, n = scales.shape
    words = np.ascontiguousarray(words).reshape(g, 128, n, -1)
    if fmt == "e4m3":
        vals = words.view(ml_dtypes.float8_e4m3fn).astype(np.float64)
    else:
        nib = np.empty((g, 128, n, 4), np.uint8)
        nib[..., 0::2] = words & 0xF
        nib[..., 1::2] = words >> 4
        vals = E2M1[nib]
    vals = vals * np.repeat(np.exp2(scales.astype(np.float64) - 127.0), 8, axis=1)[..., None]
    return vals.transpose(0, 1, 3, 2).reshape(g * 512, n)


def gelu(v):
    return 0.5 * v * (1.0 + np.tanh(np.sqrt(2.0 / np.pi) * (v + 0.044715 * v**3)))


K, T, S, H, T2, P = 1024, 2048, 512, 1024, 1024, 512

def setup_inputs():
    n = np.random.standard_normal
    s = mx_kscale(K)[:, None]
    u = mx_kscale(H)[:, None]
    d = {}
    d["tab_words"], d["tab_scales"] = pack_weight(n((K, T)) * s, "e4m3")
    d["offs"] = striped(np.random.permutation(T)[:S])
    d["offs2"] = striped(np.random.permutation(T2)[:S])
    d["offs3"] = striped(np.random.permutation(T2)[:P])
    d["wa_words"], d["wa_scales"] = pack_weight(n((K, H)) / s * u.T / K ** 0.5, "e2m1")
    d["wb"] = (1.8 * n((K, H)) / s / K ** 0.5).astype(np.float32)
    d["wc"] = (n((K, H)) / s / K ** 0.5).astype(np.float32)
    d["wgs"] = np.exp(0.3 * n((128, S))).astype(np.float32)
    d["page0"] = (n((H, T2)) * u).astype(np.float32)
    d["brief"] = (n((H, P)) * u).astype(np.float32)
    d["gain"] = (0.6 * np.exp(0.4 * n(H)) / u[:, 0] ** 2 / H ** 0.5).astype(np.float32)
    d["base"] = (0.8 * n(T2)).astype(np.float32)
    return d

def reference(tab_words, tab_scales, offs, offs2, offs3, wa_words, wa_scales, wb, wc, wgs, page0, brief, gain, base):
    v = unpack_weight(tab_words, tab_scales, "e4m3")[:, unstriped(offs)]
    a = unpack_weight(wa_words, wa_scales, "e2m1").T @ v
    b = mxq(f64(wb), 0, "e4m3").T @ v
    c = mxq(f64(wc), 0, "e4m3").T @ v
    h = a * (np.tanh(b) + np.abs(c))
    page = f64(page0).copy()
    page[:, unstriped(offs2)] = np.tile(f64(wgs), (H // 128, 1)) * h
    x = np.abs(page[:, unstriped(offs3)] - f64(brief)) * f64(gain)[:, None]
    e = mxq(page, 0, "e4m3").T @ mxq(x, 0, "e4m3")
    return np.maximum(e, f64(base)[:, None])

@@ -1,0 +1,302 @@
+from contextlib import ExitStack
+
+import concourse.mybir as mybir
+from concourse.masks import make_identity
+
+K, T, S, H, T2, PJ = 1024, 2048, 512, 1024, 1024, 512
+FLOPS = 2 * (3 * K * H * S + H * T2 * PJ)
+
+F32 = mybir.dt.float32
+BF16 = mybir.dt.bfloat16
+I32 = mybir.dt.int32
+U32 = mybir.dt.uint32
+U16 = mybir.dt.uint16
+U8 = mybir.dt.uint8
+FP8X4 = mybir.dt.float8_e4m3fn_x4
+FP4X4 = mybir.dt.float4_e2m1fn_x4
+ALU = mybir.AluOpType
+ACT = mybir.ActivationFunctionType
+
+P = 128
+PACK = 4
+PASSES = 2
+TILES = PACK * PASSES
+RAW_SLOTS = 4
+RING = 2
+F32_MAX = 3.4028234663852886e38
+BY_GPSIMD = ()
+TAIL_ENG = "ssvv"
+HEAD_ENG = "ssbb"
+ROUND = [[4], [5, 6], [7], [], [], [], [], []]
+
+
+def tile_list_sector_clue_scores_kernel(
+    tc, tab_words, tab_scales, offs, offs2, offs3, wa_words, wa_scales, wb, wc, wgs, page0, brief, gain, base, out
+):
+    nc = tc.nc
+    with ExitStack() as ctx:
+        first = ctx.enter_context(tc.tile_pool(name="first", bufs=1))
+        psum = ctx.enter_context(tc.psum_pool(name="psum", bufs=1))
+
+        lists = [first.tile([P, S // 16], U16, name="list%d" % i) for i in range(3)]
+        table_scales = first.tile([P, PASSES, T], U8, align_bytes=64)
+        table_first = first.tile([P, T], I32, align_bytes=64)
+        wa_scale = first.tile([P, PASSES, H], U8, align_bytes=64)
+        zero_bias = first.tile([P, 1], F32, align_bytes=64)
+        zero = first.tile([P, 1], F32, align_bytes=64)
+        keep = first
+
+        def tiles(name, count, shape, dtype):
+            return [keep.tile(shape, dtype, name="%s%d" % (name, i), align_bytes=64) for i in range(count)]
+
+        banks = [psum.tile([P, 512], F32, name="bank%d" % i) for i in range(8)]
+        table = [table_first] + tiles("table", PASSES - 1, [P, T], I32)
+        v_codes = tiles("v_codes", PASSES, [P, S], U32)
+        v_scales = tiles("v_scales", PASSES, [P, S], U8)
+        wa_codes = keep.tile([P, PASSES, 2 * H], U8, align_bytes=64)
+        wgs_rows = keep.tile([P, S], F32, align_bytes=64)
+        wgs_turned = keep.tile([P, S], F32, align_bytes=64)
+        weighted_turned = tiles("weighted_turned", TILES, [P, 512], F32)
+        weighted = tiles("weighted", 2, [P, S], F32)
+        raw = tiles("raw", RAW_SLOTS, [P, 2048], F32)
+        grouped = tiles("grouped", 4, [P, 2048], BF16)
+        w_codes = tiles("w_codes", 8, [P, 512], U32)
+        w_scales = tiles("w_scales", 8, [P, 512], U8)
+        page = tiles("page", TILES, [P, T2], F32)
+        briefs = tiles("brief", TILES, [P, PJ], F32)
+        tanh_b = tiles("tanh_b", RING, [P, S], F32)
+        abs_c = tiles("abs_c", RING, [P, S], F32)
+        gates = tiles("gate", 2, [P, S], F32)
+        diff = keep.tile([P, PJ], F32, align_bytes=64)
+        page_rows = keep.tile([P, PACK * T2], BF16, align_bytes=64)
+        page_grouped = keep.tile([P, PACK * T2], BF16, align_bytes=64)
+        x_rows = keep.tile([P, PACK * PJ], BF16, align_bytes=64)
+        x_grouped = keep.tile([P, PACK * PJ], BF16, align_bytes=64)
+        page_codes = tiles("page_codes", PASSES, [P, T2], U32)
+        page_scales = tiles("page_scales", PASSES, [P, T2], U8)
+        x_codes = w_codes[0:PASSES]
+        x_scales = w_scales[0:PASSES]
+        ident = keep.tile([P, P], F32, align_bytes=64)
+        base_rows = keep.tile([P, P], F32, align_bytes=64)
+        base_cols = keep.tile([P, TILES], F32, align_bytes=64)
+        gain_cols = keep.tile([P, TILES], F32, align_bytes=64)
+        not_negative = keep.tile([P, TILES], F32, align_bytes=64)
+        sign_cols = keep.tile([P, TILES], F32, align_bytes=64)
+        copier = {"v": nc.vector.tensor_copy, "s": nc.scalar.copy}
+
+        def load_scale_rows(queue, dst, src):
+            for q in range(4):
+                queue.dma_start(
+                    out=dst[32 * q : 32 * q + 4, :, :].bitcast(I32),
+                    in_=src[:, 4 * q : 4 * q + 4, :].rearrange("a q t -> q a t").bitcast(I32),
+                )
+
+        def load_weights(unit):
+            b, mat, a = unit // 4, unit % 4 // 2, unit % 2
+            nc.sync.dma_start(
+                out=raw[unit % RAW_SLOTS][:].rearrange("p (i c) -> p i c", i=PACK),
+                in_=(wb, wc)[mat][512 * a : 512 * (a + 1), 512 * b : 512 * (b + 1)].rearrange("(p i) c -> p i c", i=PACK),
+            )
+
+        def load_page(n):
+            nc.sync.dma_start(out=page[n][:], in_=page0.rearrange("(b p t) m -> b t p m", b=PASSES, t=PACK)[n // PACK, n % PACK])
+
+        def load_brief(n):
+            nc.sync.dma_start(out=briefs[n][:], in_=brief.rearrange("(b p t) j -> b t p j", b=PASSES, t=PACK)[n // PACK, n % PACK])
+
+        def round_weights(unit, engines):
+            dst = grouped[unit % 4][:].rearrange("p (t q i) -> p q i t", t=PACK, i=PACK)
+            src = raw[unit % RAW_SLOTS][:].rearrange("p (i q t) -> p q i t", t=PACK, i=PACK)
+            if engines == "b":
+                nc.scalar.copy(out=dst[:, 0:48], in_=src[:, 0:48])
+                nc.vector.tensor_copy(out=dst[:, 48:128], in_=src[:, 48:128])
+            else:
+                copier[engines](out=dst, in_=src)
+
+        def quantise(codes, scales, values):
+            nc.vector.quantize_mx(out=codes.bitcast(FP8X4), scales=scales, in_=values)
+
+        def quantise_weights(unit):
+            pieces = 2 if unit == 3 else 1
+            for i in range(pieces):
+                lo, hi = 512 // pieces * i, 512 // pieces * (i + 1)
+                quantise(w_codes[unit][:, lo:hi], w_scales[unit][:, lo:hi], grouped[unit % 4][:, 4 * lo : 4 * hi])
+
+        def products_bc(n):
+            cols = slice(P * (n % PACK), P * (n % PACK + 1))
+            for mat, (dst, func) in enumerate(((tanh_b, ACT.Tanh), (abs_c, ACT.Abs))):
+                for a in range(PASSES):
+                    unit = 4 * (n // PACK) + 2 * mat + a
+                    nc.tensor.matmul_mx(
+                        banks[(n + mat) % 2][:], lhsT=w_codes[unit][:, cols].bitcast(FP8X4), lhsT_scale=w_scales[unit][:, cols],
+                        rhs=v_codes[a][:].bitcast(FP8X4), rhs_scale=v_scales[a][:], start=(a == 0), stop=(a == PASSES - 1),
+                    )
+                nc.scalar.activation(dst[n % RING][:], banks[(n + mat) % 2][:], func, bias=zero_bias[:])
+
+        def product_a_turned(b, part, bank):
+            cols = slice(P * part, P * (part + 1))
+            for a in range(PASSES):
+                nc.tensor.matmul_mx(
+                    bank[:], lhsT=v_codes[a][:, cols].bitcast(FP8X4), lhsT_scale=v_scales[a][:, cols],
+                    rhs=wa_codes[:, a, 1024 * b : 1024 * (b + 1)].bitcast(FP4X4), rhs_scale=wa_scale[:, a, 512 * b : 512 * (b + 1)],
+                    start=(a == 0), stop=(a == PASSES - 1),
+                )
+            factors = wgs_turned[:, cols].rearrange("j (t q) -> j t q", t=PACK).unsqueeze(2).to_broadcast([P, PACK, 4, 32])
+            nc.vector.tensor_tensor(
+                weighted_turned[4 * b + part][:].rearrange("j (t h q) -> j t h q", t=PACK, h=4),
+                bank[:].rearrange("j (h q t) -> j t h q", t=PACK, h=4), factors, ALU.mult,
+            )
+
+        def turn_weighted(n):
+            for part in range(4):
+                src = weighted_turned[4 * (n // PACK) + part]
+                nc.tensor.transpose(banks[2][:, P * part : P * (part + 1)], src[:, P * (n % PACK) : P * (n % PACK + 1)], ident[:])
+            nc.scalar.copy(out=weighted_a(n), in_=banks[2][:])
+
+        def weighted_a(n):
+            return weighted[n % 2][:]
+
+        def add_gate(n):
+            nc.vector.tensor_tensor(gates[n % 2][:], tanh_b[n % RING][:], abs_c[n % RING][:], ALU.add)
+
+        def put_columns(n):
+            nc.vector.tensor_tensor(page[n][:].indirect(lists[1][:]), gates[n % 2][:], weighted_a(n), ALU.mult)
+
+        def fetch_columns(n):
+            nc.vector.tensor_tensor(diff[:], page[n][:].indirect(lists[2][:]), briefs[n][:], ALU.subtract)
+
+        def round_page(n):
+            t = n % PACK
+            nc.scalar.activation(page_rows[:, T2 * t : T2 * (t + 1)], page[n][:], ACT.Copy, scale=sign_cols[:, n : n + 1])
+
+        def round_x(n):
+            t = n % PACK
+            nc.scalar.activation(x_rows[:, PJ * t : PJ * (t + 1)], diff[:], ACT.Abs, bias=zero_bias[:], scale=gain_cols[:, n : n + 1])
+
+        def interleave(engine, dst, src, lo, hi):
+            copier[engine](
+                out=dst[:, PACK * lo : PACK * hi].rearrange("p (c i t) -> p c t i", i=4, t=PACK),
+                in_=src[:].rearrange("p (t c) -> p t c", t=PACK)[:, :, lo:hi].rearrange("p t (c i) -> p c t i", i=4),
+            )
+
+        def score_pass(b, mt):
+            rows = slice(P * mt, P * (mt + 1))
+            nc.tensor.matmul_mx(
+                banks[(mt + 3) % 8][:], lhsT=page_codes[b][:, rows].bitcast(FP8X4), lhsT_scale=page_scales[b][:, rows],
+                rhs=x_codes[b][:].bitcast(FP8X4), rhs_scale=x_scales[b][:], start=(b == 0), stop=(b == PASSES - 1),
+            )
+
+        def finish(mt):
+            bank, floor, result = banks[(mt + 3) % 8], base_cols[:, mt : mt + 1], briefs[mt]
+            if mt in BY_GPSIMD:
+                nc.scalar.copy(out=result[:], in_=bank[:])
+                nc.gpsimd.tensor_scalar(result[:], result[:], F32_MAX, floor, ALU.min, ALU.max)
+            else:
+                nc.vector.tensor_scalar(result[:], bank[:], floor, None, ALU.max)
+            nc.sync.dma_start(out=out[P * mt : P * (mt + 1), :], in_=result[:])
+
+        nc.gpsimd.memset(zero[:], 0.0)
+        nc.scalar.activation(zero_bias[:], zero[:], ACT.Tanh)
+        nc.vector.memset(table_scales[:].rearrange("p a t -> p (a t)").bitcast(I32), 0)
+        nc.vector.memset(wa_scale[:].rearrange("p a t -> p (a t)").bitcast(I32), 0)
+        make_identity(nc, ident[:])
+        nc.gpsimd.memset(base_rows[:], 0.0)
+
+        def load_table(a):
+            nc.sync.dma_start(out=table[a][:], in_=tab_words[a].rearrange("p t i -> p (t i)").bitcast(I32))
+
+        nc.sync.dma_start(lists[0][:], offs)
+        load_table(0)
+        load_scale_rows(nc.sync, table_scales, tab_scales)
+        load_table(1)
+        nc.sync.dma_start(out=wgs_rows[:], in_=wgs)
+        nc.sync.dma_start(out=wa_codes[:].bitcast(I32), in_=wa_words.rearrange("a p n -> p a n").bitcast(I32))
+        load_scale_rows(nc.sync, wa_scale, wa_scales)
+        for unit in range(4):
+            load_weights(unit)
+        nc.sync.dma_start(lists[1][:], offs2)
+        load_page(0)
+        nc.sync.dma_start(lists[2][:], offs3)
+        nc.sync.dma_start(out=gain_cols[:].rearrange("p (b t) -> p b t", t=PACK), in_=gain.rearrange("(b p t) -> p b t", p=P, t=PACK))
+        nc.sync.dma_start(out=base_rows[0:TILES, :], in_=base.rearrange("(n p) -> n p", p=P))
+
+        for a in range(PASSES):
+            nc.vector.tensor_copy(v_scales[a][:], table_scales[:, a, :].indirect(lists[0][:]))
+        for a in range(PASSES):
+            nc.vector.tensor_copy(v_codes[a][:], table[a][:].bitcast(U32).indirect(lists[0][:]))
+
+        for part in range(4):
+            nc.tensor.transpose(banks[2][:, P * part : P * (part + 1)], wgs_rows[:, P * part : P * (part + 1)], ident[:])
+        nc.scalar.copy(
+            out=wgs_turned[:].rearrange("j (c t q) -> j c t q", c=4, t=PACK), in_=banks[2][:].rearrange("j (c q t) -> j c t q", c=4, t=PACK)
+        )
+        for unit in range(4):
+            round_weights(unit, HEAD_ENG[unit])
+            quantise_weights(unit)
+            load_weights(unit + 4)
+            if unit != 2:
+                load_brief(min(unit, 2))
+                load_page(min(unit, 2) + 1)
+        for n in range(3, TILES):
+            load_brief(n)
+            if n + 1 < TILES:
+                load_page(n + 1)
+        products_bc(0)
+        add_gate(0)
+        for b in range(PASSES):
+            for part in range(4):
+                product_a_turned(b, part, banks[3 + (4 * b + part) % 5])
+            if b == 0:
+                turn_weighted(0)
+        nc.gpsimd.tensor_scalar(not_negative[:], gain_cols[:], 0.0, None, ALU.is_ge)
+        nc.gpsimd.tensor_scalar(sign_cols[:], not_negative[:], 2.0, -1.0, ALU.mult, ALU.add)
+
+        last = TILES - 1
+        for n in range(TILES):
+            put_columns(n)
+            if n == PACK - 1:
+                for m in range(PACK - 1):
+                    round_page(m)
+            if n < last:
+                products_bc(n + 1)
+                add_gate(n + 1)
+            if n >= 1:
+                round_x(n - 1)
+            fetch_columns(n)
+            for unit in ROUND[n]:
+                round_weights(unit, "s")
+                quantise_weights(unit)
+            if n == PACK:
+                round_page(PACK - 1)
+                interleave("s", x_grouped, x_rows, 0, PJ)
+                quantise(x_codes[0][:], x_scales[0][:], x_grouped[:])
+            if n == PACK + 1:
+                for half in range(2):
+                    interleave("s", page_grouped, page_rows, 512 * half, 512 * (half + 1))
+                    quantise(page_codes[0][:, 512 * half : 512 * (half + 1)], page_scales[0][:, 512 * half : 512 * (half + 1)], page_grouped[:, 2048 * half : 2048 * (half + 1)])
+            if n == PACK + 2:
+                round_page(n - 2)
+                round_page(n - 1)
+                nc.tensor.transpose(banks[7][:, 0:P], base_rows[:], ident[:])
+                nc.scalar.copy(out=base_cols[:], in_=banks[7][:, 0:TILES])
+            if n < last:
+                turn_weighted(n + 1)
+        round_page(last - 1)
+        round_page(last)
+        round_x(last)
+        for mt in range(TILES):
+            score_pass(0, mt)
+        interleave("v", x_grouped, x_rows, 0, PJ)
+        order = (2, 3, 0, 1)
+        for quarter in order:
+            interleave(TAIL_ENG[quarter], page_grouped, page_rows, 256 * quarter, 256 * (quarter + 1))
+        quantise(x_codes[1][:], x_scales[1][:], x_grouped[:])
+        for quarter in order:
+            cols = slice(256 * quarter, 256 * (quarter + 1))
+            quantise(page_codes[1][:, cols], page_scales[1][:, cols], page_grouped[:, 1024 * quarter : 1024 * (quarter + 1)])
+        for quarter in order:
+            for mt in (2 * quarter, 2 * quarter + 1):
+                score_pass(1, mt)
+        for quarter in order:
+            for mt in (2 * quarter, 2 * quarter + 1):
+                finish(mt)

@@ -23,6 +23,11 @@ PASSES = 2
 TILES = PACK * PASSES
 RAW_SLOTS = 4
 RING = 2
+LATE_FROM = 6
+EARLY_PAGES = 1
+X0_ENG = "s"
+HALVES = [[], [0, 1]]
+LOADS = "w4 b0 p1 w5 w6 b1 p2 w7 b2 b3 p3 p4 b4 p5 b5 p6 b6 p7 b7"
 F32_MAX = 3.4028234663852886e38
 BY_GPSIMD = ()
 TAIL_ENG = "ssvv"
@@ -66,9 +71,9 @@ def tile_list_sector_clue_scores_kernel(
         briefs = tiles("brief", TILES, [P, PJ], F32)
         tanh_b = tiles("tanh_b", RING, [P, S], F32)
         abs_c = tiles("abs_c", RING, [P, S], F32)
-        gates = tiles("gate", 2, [P, S], F32)
+        gates = tiles("gate", 3, [P, S], F32)
         diff = keep.tile([P, PJ], F32, align_bytes=64)
-        page_rows = keep.tile([P, PACK * T2], BF16, align_bytes=64)
+        page_rows = raw[RAW_SLOTS - 1][:].bitcast(BF16)
         page_grouped = keep.tile([P, PACK * T2], BF16, align_bytes=64)
         x_rows = keep.tile([P, PACK * PJ], BF16, align_bytes=64)
         x_grouped = keep.tile([P, PACK * PJ], BF16, align_bytes=64)
@@ -104,8 +109,11 @@ def tile_list_sector_clue_scores_kernel(
         def load_brief(n):
             nc.sync.dma_start(out=briefs[n][:], in_=brief.rearrange("(b p t) j -> b t p j", b=PASSES, t=PACK)[n // PACK, n % PACK])
 
+        def staged(unit):
+            return grouped[unit % 4][:]
+
         def round_weights(unit, engines):
-            dst = grouped[unit % 4][:].rearrange("p (t q i) -> p q i t", t=PACK, i=PACK)
+            dst = staged(unit).rearrange("p (t q i) -> p q i t", t=PACK, i=PACK)
             src = raw[unit % RAW_SLOTS][:].rearrange("p (i q t) -> p q i t", t=PACK, i=PACK)
             if engines == "b":
                 nc.scalar.copy(out=dst[:, 0:48], in_=src[:, 0:48])
@@ -120,7 +128,7 @@ def tile_list_sector_clue_scores_kernel(
             pieces = 2 if unit == 3 else 1
             for i in range(pieces):
                 lo, hi = 512 // pieces * i, 512 // pieces * (i + 1)
-                quantise(w_codes[unit][:, lo:hi], w_scales[unit][:, lo:hi], grouped[unit % 4][:, 4 * lo : 4 * hi])
+                quantise(w_codes[unit][:, lo:hi], w_scales[unit][:, lo:hi], staged(unit)[:, 4 * lo : 4 * hi])
 
         def products_bc(n):
             cols = slice(P * (n % PACK), P * (n % PACK + 1))
@@ -148,19 +156,20 @@ def tile_list_sector_clue_scores_kernel(
             )
 
         def turn_weighted(n):
+            bank = banks[(n + 1) % 2 if 0 < n <= PACK else 2]
             for part in range(4):
                 src = weighted_turned[4 * (n // PACK) + part]
-                nc.tensor.transpose(banks[2][:, P * part : P * (part + 1)], src[:, P * (n % PACK) : P * (n % PACK + 1)], ident[:])
-            nc.scalar.copy(out=weighted_a(n), in_=banks[2][:])
+                nc.tensor.transpose(bank[:, P * part : P * (part + 1)], src[:, P * (n % PACK) : P * (n % PACK + 1)], ident[:])
+            nc.scalar.copy(out=weighted_a(n), in_=bank[:])
 
         def weighted_a(n):
-            return weighted[n % 2][:]
+            return weighted[n % 2][:] if n else grouped[1][:, 0:1024].bitcast(F32)
 
         def add_gate(n):
-            nc.vector.tensor_tensor(gates[n % 2][:], tanh_b[n % RING][:], abs_c[n % RING][:], ALU.add)
+            nc.vector.tensor_tensor(gates[n % 3][:], tanh_b[n % RING][:], abs_c[n % RING][:], ALU.add)
 
         def put_columns(n):
-            nc.vector.tensor_tensor(page[n][:].indirect(lists[1][:]), gates[n % 2][:], weighted_a(n), ALU.mult)
+            nc.vector.tensor_tensor(page[n][:].indirect(lists[1][:]), gates[n % 3][:], weighted_a(n), ALU.mult)
 
         def fetch_columns(n):
             nc.vector.tensor_tensor(diff[:], page[n][:].indirect(lists[2][:]), briefs[n][:], ALU.subtract)
@@ -176,7 +185,7 @@ def tile_list_sector_clue_scores_kernel(
         def interleave(engine, dst, src, lo, hi):
             copier[engine](
                 out=dst[:, PACK * lo : PACK * hi].rearrange("p (c i t) -> p c t i", i=4, t=PACK),
-                in_=src[:].rearrange("p (t c) -> p t c", t=PACK)[:, :, lo:hi].rearrange("p t (c i) -> p c t i", i=4),
+                in_=src.rearrange("p (t c) -> p t c", t=PACK)[:, :, lo:hi].rearrange("p t (c i) -> p c t i", i=4),
             )
 
         def score_pass(b, mt):
@@ -209,9 +218,9 @@ def tile_list_sector_clue_scores_kernel(
         load_table(0)
         load_scale_rows(nc.sync, table_scales, tab_scales)
         load_table(1)
+        load_scale_rows(nc.sync, wa_scale, wa_scales)
         nc.sync.dma_start(out=wgs_rows[:], in_=wgs)
         nc.sync.dma_start(out=wa_codes[:].bitcast(I32), in_=wa_words.rearrange("a p n -> p a n").bitcast(I32))
-        load_scale_rows(nc.sync, wa_scale, wa_scales)
         for unit in range(4):
             load_weights(unit)
         nc.sync.dma_start(lists[1][:], offs2)
@@ -233,14 +242,8 @@ def tile_list_sector_clue_scores_kernel(
         for unit in range(4):
             round_weights(unit, HEAD_ENG[unit])
             quantise_weights(unit)
-            load_weights(unit + 4)
-            if unit != 2:
-                load_brief(min(unit, 2))
-                load_page(min(unit, 2) + 1)
-        for n in range(3, TILES):
-            load_brief(n)
-            if n + 1 < TILES:
-                load_page(n + 1)
+        for step in LOADS.split():
+            {"w": load_weights, "p": load_page, "b": load_brief}[step[0]](int(step[1]))
         products_bc(0)
         add_gate(0)
         for b in range(PASSES):
@@ -255,38 +258,46 @@ def tile_list_sector_clue_scores_kernel(
         for n in range(TILES):
             put_columns(n)
             if n == PACK - 1:
-                for m in range(PACK - 1):
+                for m in range(EARLY_PAGES):
                     round_page(m)
             if n < last:
                 products_bc(n + 1)
                 add_gate(n + 1)
+            if n < PACK:
+                turn_weighted(n + 1)
             if n >= 1:
                 round_x(n - 1)
+            if PACK <= n < LATE_FROM:
+                turn_weighted(n + 1)
             fetch_columns(n)
             for unit in ROUND[n]:
                 round_weights(unit, "s")
                 quantise_weights(unit)
+            if n == PACK - 1:
+                for m in range(EARLY_PAGES, PACK - 1):
+                    round_page(m)
             if n == PACK:
-                round_page(PACK - 1)
-                interleave("s", x_grouped, x_rows, 0, PJ)
+                interleave(X0_ENG, x_grouped, x_rows[:], 0, PJ)
                 quantise(x_codes[0][:], x_scales[0][:], x_grouped[:])
-            if n == PACK + 1:
-                for half in range(2):
+                round_page(PACK - 1)
+            if n in (PACK, PACK + 1):
+                for half in HALVES[n - PACK]:
                     interleave("s", page_grouped, page_rows, 512 * half, 512 * (half + 1))
                     quantise(page_codes[0][:, 512 * half : 512 * (half + 1)], page_scales[0][:, 512 * half : 512 * (half + 1)], page_grouped[:, 2048 * half : 2048 * (half + 1)])
             if n == PACK + 2:
-                round_page(n - 2)
-                round_page(n - 1)
                 nc.tensor.transpose(banks[7][:, 0:P], base_rows[:], ident[:])
                 nc.scalar.copy(out=base_cols[:], in_=banks[7][:, 0:TILES])
-            if n < last:
+            if LATE_FROM <= n < last:
                 turn_weighted(n + 1)
+            if n == PACK + 2:
+                round_page(n - 2)
+                round_page(n - 1)
         round_page(last - 1)
         round_page(last)
         round_x(last)
         for mt in range(TILES):
             score_pass(0, mt)
-        interleave("v", x_grouped, x_rows, 0, PJ)
+        interleave("v", x_grouped, x_rows[:], 0, PJ)
         order = (2, 3, 0, 1)
         for quarter in order:
             interleave(TAIL_ENG[quarter], page_grouped, page_rows, 256 * quarter, 256 * (quarter + 1))

@@ -19,20 +19,15 @@ ACT = mybir.ActivationFunctionType
 
 P = 128
 PACK = 4
-PASSES = 2
+SPAN = P * PACK
+PASSES = K // SPAN
 TILES = PACK * PASSES
-RAW_SLOTS = 4
-RING = 2
-LATE_FROM = 6
-EARLY_PAGES = 1
-X0_ENG = "s"
-HALVES = [[], [0, 1]]
-LOADS = "w4 b0 p1 w5 w6 b1 p2 w7 b2 b3 p3 p4 b4 p5 b5 p6 b6 p7 b7"
-F32_MAX = 3.4028234663852886e38
-BY_GPSIMD = ()
-TAIL_ENG = "ssvv"
-HEAD_ENG = "ssbb"
-ROUND = [[4], [5, 6], [7], [], [], [], [], []]
+PARTS = S // P
+BANKS = 8
+CHUNKS = 2 * PASSES
+SCALAR_GROUPS = 48
+LATER_CHUNKS = ((4,), (5, 6), (7,))
+BRIEF_LAG = 2
 
 
 def tile_list_sector_clue_scores_kernel(
@@ -40,139 +35,148 @@ def tile_list_sector_clue_scores_kernel(
 ):
     nc = tc.nc
     with ExitStack() as ctx:
-        first = ctx.enter_context(tc.tile_pool(name="first", bufs=1))
+        sbuf = ctx.enter_context(tc.tile_pool(name="sbuf", bufs=1))
         psum = ctx.enter_context(tc.psum_pool(name="psum", bufs=1))
 
-        lists = [first.tile([P, S // 16], U16, name="list%d" % i) for i in range(3)]
-        table_scales = first.tile([P, PASSES, T], U8, align_bytes=64)
-        table_first = first.tile([P, T], I32, align_bytes=64)
-        wa_scale = first.tile([P, PASSES, H], U8, align_bytes=64)
-        zero_bias = first.tile([P, 1], F32, align_bytes=64)
-        zero = first.tile([P, 1], F32, align_bytes=64)
-        keep = first
-
         def tiles(name, count, shape, dtype):
-            return [keep.tile(shape, dtype, name="%s%d" % (name, i), align_bytes=64) for i in range(count)]
+            return [sbuf.tile(shape, dtype, name="%s%d" % (name, i), align_bytes=64) for i in range(count)]
 
-        banks = [psum.tile([P, 512], F32, name="bank%d" % i) for i in range(8)]
-        table = [table_first] + tiles("table", PASSES - 1, [P, T], I32)
+        table_list, put_list, fetch_list = [sbuf.tile([P, S // 16], U16, name="list%d" % i) for i in range(3)]
+        table_scales = sbuf.tile([P, PASSES, T], U8, align_bytes=64)
+        wa_scale = sbuf.tile([P, PASSES, H], U8, align_bytes=64)
+        zero = sbuf.tile([P, 1], F32, align_bytes=64)
+        zero_bias = sbuf.tile([P, 1], F32, align_bytes=64)
+        banks = [psum.tile([P, 512], F32, name="bank%d" % i) for i in range(BANKS)]
+        table = tiles("table", PASSES, [P, T], I32)
         v_codes = tiles("v_codes", PASSES, [P, S], U32)
         v_scales = tiles("v_scales", PASSES, [P, S], U8)
-        wa_codes = keep.tile([P, PASSES, 2 * H], U8, align_bytes=64)
-        wgs_rows = keep.tile([P, S], F32, align_bytes=64)
-        wgs_turned = keep.tile([P, S], F32, align_bytes=64)
-        weighted_turned = tiles("weighted_turned", TILES, [P, 512], F32)
-        weighted = tiles("weighted", 2, [P, S], F32)
-        raw = tiles("raw", RAW_SLOTS, [P, 2048], F32)
-        grouped = tiles("grouped", 4, [P, 2048], BF16)
-        w_codes = tiles("w_codes", 8, [P, 512], U32)
-        w_scales = tiles("w_scales", 8, [P, 512], U8)
+        wa_codes = sbuf.tile([P, PASSES, 2 * H], U8, align_bytes=64)
+        wgs_rows = sbuf.tile([P, S], F32, align_bytes=64)
+        wgs_turned = sbuf.tile([P, S], F32, align_bytes=64)
+        weighted_turned = tiles("weighted_turned", PASSES * PARTS, [P, SPAN], F32)
+        weighted_pair = tiles("weighted_pair", 2, [P, S], F32)
+        raw = tiles("raw", CHUNKS, [P, PACK * SPAN], F32)
+        rounded = tiles("rounded", CHUNKS, [P, PACK * SPAN], BF16)
+        w_codes = tiles("w_codes", PASSES * CHUNKS, [P, SPAN], U32)
+        w_scales = tiles("w_scales", PASSES * CHUNKS, [P, SPAN], U8)
         page = tiles("page", TILES, [P, T2], F32)
-        briefs = tiles("brief", TILES, [P, PJ], F32)
-        tanh_b = tiles("tanh_b", RING, [P, S], F32)
-        abs_c = tiles("abs_c", RING, [P, S], F32)
-        gates = tiles("gate", 3, [P, S], F32)
-        diff = keep.tile([P, PJ], F32, align_bytes=64)
-        page_rows = raw[RAW_SLOTS - 1][:].bitcast(BF16)
-        page_grouped = keep.tile([P, PACK * T2], BF16, align_bytes=64)
-        x_rows = keep.tile([P, PACK * PJ], BF16, align_bytes=64)
-        x_grouped = keep.tile([P, PACK * PJ], BF16, align_bytes=64)
+        briefs = tiles("briefs", TILES, [P, PJ], F32)
+        tanh_b = tiles("tanh_b", 2, [P, S], F32)
+        abs_c = tiles("abs_c", 2, [P, S], F32)
+        sums = tiles("sums", 3, [P, S], F32)
+        diff = sbuf.tile([P, PJ], F32, align_bytes=64)
+        page_rows = raw[CHUNKS - 1][:].bitcast(BF16)
+        page_words = sbuf.tile([P, PACK * T2], BF16, align_bytes=64)
+        x_rows = sbuf.tile([P, PACK * PJ], BF16, align_bytes=64)
+        x_words = sbuf.tile([P, PACK * PJ], BF16, align_bytes=64)
         page_codes = tiles("page_codes", PASSES, [P, T2], U32)
         page_scales = tiles("page_scales", PASSES, [P, T2], U8)
         x_codes = w_codes[0:PASSES]
         x_scales = w_scales[0:PASSES]
-        ident = keep.tile([P, P], F32, align_bytes=64)
-        base_rows = keep.tile([P, P], F32, align_bytes=64)
-        base_cols = keep.tile([P, TILES], F32, align_bytes=64)
-        gain_cols = keep.tile([P, TILES], F32, align_bytes=64)
-        not_negative = keep.tile([P, TILES], F32, align_bytes=64)
-        sign_cols = keep.tile([P, TILES], F32, align_bytes=64)
-        copier = {"v": nc.vector.tensor_copy, "s": nc.scalar.copy}
+        ident = sbuf.tile([P, P], F32, align_bytes=64)
+        base_rows = sbuf.tile([P, P], F32, align_bytes=64)
+        base_cols = sbuf.tile([P, TILES], F32, align_bytes=64)
+        gain_cols = sbuf.tile([P, TILES], F32, align_bytes=64)
+        not_negative = sbuf.tile([P, TILES], F32, align_bytes=64)
+        sign_cols = sbuf.tile([P, TILES], F32, align_bytes=64)
 
-        def load_scale_rows(queue, dst, src):
-            for q in range(4):
-                queue.dma_start(
-                    out=dst[32 * q : 32 * q + 4, :, :].bitcast(I32),
-                    in_=src[:, 4 * q : 4 * q + 4, :].rearrange("a q t -> q a t").bitcast(I32),
+
+        def load_table(a):
+            nc.sync.dma_start(out=table[a][:], in_=tab_words[a].rearrange("p c i -> p (c i)").bitcast(I32))
+
+        def load_scale_rows(dst, src):
+            for quad in range(4):
+                nc.sync.dma_start(
+                    out=dst[32 * quad : 32 * quad + 4, :, :].bitcast(I32),
+                    in_=src[:, 4 * quad : 4 * quad + 4, :].rearrange("a s c -> s a c").bitcast(I32),
                 )
 
-        def load_weights(unit):
-            b, mat, a = unit // 4, unit % 4 // 2, unit % 2
+        def load_chunk(chunk):
+            g, matrix, a = chunk // CHUNKS, chunk % CHUNKS // PASSES, chunk % PASSES
+            src = (wb, wc)[matrix][SPAN * a : SPAN * (a + 1), SPAN * g : SPAN * (g + 1)]
             nc.sync.dma_start(
-                out=raw[unit % RAW_SLOTS][:].rearrange("p (i c) -> p i c", i=PACK),
-                in_=(wb, wc)[mat][512 * a : 512 * (a + 1), 512 * b : 512 * (b + 1)].rearrange("(p i) c -> p i c", i=PACK),
+                out=raw[chunk % CHUNKS][:].rearrange("p (i c) -> p i c", i=PACK), in_=src.rearrange("(p i) c -> p i c", i=PACK)
             )
 
+        def tile_rows(src, n):
+            return src.rearrange("(g p t) c -> g t p c", g=PASSES, t=PACK)[n // PACK, n % PACK]
+
         def load_page(n):
-            nc.sync.dma_start(out=page[n][:], in_=page0.rearrange("(b p t) m -> b t p m", b=PASSES, t=PACK)[n // PACK, n % PACK])
+            nc.sync.dma_start(out=page[n][:], in_=tile_rows(page0, n))
 
         def load_brief(n):
-            nc.sync.dma_start(out=briefs[n][:], in_=brief.rearrange("(b p t) j -> b t p j", b=PASSES, t=PACK)[n // PACK, n % PACK])
+            nc.sync.dma_start(out=briefs[n][:], in_=tile_rows(brief, n))
 
-        def staged(unit):
-            return grouped[unit % 4][:]
-
-        def round_weights(unit, engines):
-            dst = staged(unit).rearrange("p (t q i) -> p q i t", t=PACK, i=PACK)
-            src = raw[unit % RAW_SLOTS][:].rearrange("p (i q t) -> p q i t", t=PACK, i=PACK)
-            if engines == "b":
-                nc.scalar.copy(out=dst[:, 0:48], in_=src[:, 0:48])
-                nc.vector.tensor_copy(out=dst[:, 48:128], in_=src[:, 48:128])
-            else:
-                copier[engines](out=dst, in_=src)
 
         def quantise(codes, scales, values):
             nc.vector.quantize_mx(out=codes.bitcast(FP8X4), scales=scales, in_=values)
 
-        def quantise_weights(unit):
-            pieces = 2 if unit == 3 else 1
-            for i in range(pieces):
-                lo, hi = 512 // pieces * i, 512 // pieces * (i + 1)
-                quantise(w_codes[unit][:, lo:hi], w_scales[unit][:, lo:hi], staged(unit)[:, 4 * lo : 4 * hi])
+        def chunk_views(chunk):
+            dst = rounded[chunk % CHUNKS][:].rearrange("p (t q i) -> p q i t", t=PACK, i=PACK)
+            src = raw[chunk % CHUNKS][:].rearrange("p (i q t) -> p q i t", t=PACK, i=PACK)
+            return dst, src
 
-        def products_bc(n):
+        def round_chunk(chunk):
+            dst, src = chunk_views(chunk)
+            nc.scalar.copy(out=dst, in_=src)
+
+        def round_chunk_on_two_engines(chunk):
+            dst, src = chunk_views(chunk)
+            nc.scalar.copy(out=dst[:, :SCALAR_GROUPS], in_=src[:, :SCALAR_GROUPS])
+            nc.vector.tensor_copy(out=dst[:, SCALAR_GROUPS:], in_=src[:, SCALAR_GROUPS:])
+
+        def quantise_chunk(chunk, lo, hi):
+            quantise(w_codes[chunk][:, lo:hi], w_scales[chunk][:, lo:hi], rounded[chunk % CHUNKS][:, PACK * lo : PACK * hi])
+
+        def product(n, matrix, bank, lo, hi):
             cols = slice(P * (n % PACK), P * (n % PACK + 1))
-            for mat, (dst, func) in enumerate(((tanh_b, ACT.Tanh), (abs_c, ACT.Abs))):
-                for a in range(PASSES):
-                    unit = 4 * (n // PACK) + 2 * mat + a
-                    nc.tensor.matmul_mx(
-                        banks[(n + mat) % 2][:], lhsT=w_codes[unit][:, cols].bitcast(FP8X4), lhsT_scale=w_scales[unit][:, cols],
-                        rhs=v_codes[a][:].bitcast(FP8X4), rhs_scale=v_scales[a][:], start=(a == 0), stop=(a == PASSES - 1),
-                    )
-                nc.scalar.activation(dst[n % RING][:], banks[(n + mat) % 2][:], func, bias=zero_bias[:])
-
-        def product_a_turned(b, part, bank):
-            cols = slice(P * part, P * (part + 1))
+            dst, func = ((tanh_b, ACT.Tanh), (abs_c, ACT.Abs))[matrix]
             for a in range(PASSES):
+                chunk = CHUNKS * (n // PACK) + PASSES * matrix + a
                 nc.tensor.matmul_mx(
-                    bank[:], lhsT=v_codes[a][:, cols].bitcast(FP8X4), lhsT_scale=v_scales[a][:, cols],
-                    rhs=wa_codes[:, a, 1024 * b : 1024 * (b + 1)].bitcast(FP4X4), rhs_scale=wa_scale[:, a, 512 * b : 512 * (b + 1)],
+                    bank[:, lo:hi], lhsT=w_codes[chunk][:, cols].bitcast(FP8X4), lhsT_scale=w_scales[chunk][:, cols],
+                    rhs=v_codes[a][:, lo:hi].bitcast(FP8X4), rhs_scale=v_scales[a][:, lo:hi],
                     start=(a == 0), stop=(a == PASSES - 1),
                 )
-            factors = wgs_turned[:, cols].rearrange("j (t q) -> j t q", t=PACK).unsqueeze(2).to_broadcast([P, PACK, 4, 32])
+            nc.scalar.activation(dst[n % 2][:, lo:hi], bank[:, lo:hi], func, bias=zero_bias[:])
+
+        def add_products(n, lo, hi):
+            nc.vector.tensor_tensor(sums[n % 3][:, lo:hi], tanh_b[n % 2][:, lo:hi], abs_c[n % 2][:, lo:hi], ALU.add)
+
+        def weigh_a_turned(g, part, bank):
+            entries = slice(P * part, P * (part + 1))
+            for a in range(PASSES):
+                nc.tensor.matmul_mx(
+                    bank[:], lhsT=v_codes[a][:, entries].bitcast(FP8X4), lhsT_scale=v_scales[a][:, entries],
+                    rhs=wa_codes[:, a, 2 * SPAN * g : 2 * SPAN * (g + 1)].bitcast(FP4X4),
+                    rhs_scale=wa_scale[:, a, SPAN * g : SPAN * (g + 1)],
+                    start=(a == 0), stop=(a == PASSES - 1),
+                )
+            factors = wgs_turned[:, entries].rearrange("j (t q) -> j t q", t=PACK).unsqueeze(2).to_broadcast([P, PACK, 4, 32])
             nc.vector.tensor_tensor(
-                weighted_turned[4 * b + part][:].rearrange("j (t h q) -> j t h q", t=PACK, h=4),
-                bank[:].rearrange("j (h q t) -> j t h q", t=PACK, h=4), factors, ALU.mult,
+                weighted_turned[PARTS * g + part][:].rearrange("j (t u q) -> j t u q", t=PACK, u=4),
+                bank[:].rearrange("j (u q t) -> j t u q", t=PACK, u=4), factors, ALU.mult,
             )
 
+        def weighted(n):
+            if n % PACK == 0:
+                return rounded[CHUNKS - 1 if n else 1][:, 0 : 2 * S].bitcast(F32)
+            return weighted_pair[n % 2][:]
+
         def turn_weighted(n):
-            bank = banks[(n + 1) % 2 if 0 < n <= PACK else 2]
-            for part in range(4):
-                src = weighted_turned[4 * (n // PACK) + part]
+            bank = banks[(n + 1) % 2 if 0 < n < PACK else 2]
+            for part in range(PARTS):
+                src = weighted_turned[PARTS * (n // PACK) + part]
                 nc.tensor.transpose(bank[:, P * part : P * (part + 1)], src[:, P * (n % PACK) : P * (n % PACK + 1)], ident[:])
-            nc.scalar.copy(out=weighted_a(n), in_=bank[:])
+            nc.scalar.copy(out=weighted(n), in_=bank[:])
 
-        def weighted_a(n):
-            return weighted[n % 2][:] if n else grouped[1][:, 0:1024].bitcast(F32)
+        def put_columns(n, lo, hi):
+            offsets = put_list[:, lo // 16 : hi // 16]
+            nc.vector.tensor_tensor(page[n][:].indirect(offsets), sums[n % 3][:, lo:hi], weighted(n)[:, lo:hi], ALU.mult)
 
-        def add_gate(n):
-            nc.vector.tensor_tensor(gates[n % 3][:], tanh_b[n % RING][:], abs_c[n % RING][:], ALU.add)
-
-        def put_columns(n):
-            nc.vector.tensor_tensor(page[n][:].indirect(lists[1][:]), gates[n % 3][:], weighted_a(n), ALU.mult)
 
         def fetch_columns(n):
-            nc.vector.tensor_tensor(diff[:], page[n][:].indirect(lists[2][:]), briefs[n][:], ALU.subtract)
+            nc.vector.tensor_tensor(diff[:], page[n][:].indirect(fetch_list[:]), briefs[n][:], ALU.subtract)
 
         def round_page(n):
             t = n % PACK
@@ -180,134 +184,161 @@ def tile_list_sector_clue_scores_kernel(
 
         def round_x(n):
             t = n % PACK
-            nc.scalar.activation(x_rows[:, PJ * t : PJ * (t + 1)], diff[:], ACT.Abs, bias=zero_bias[:], scale=gain_cols[:, n : n + 1])
-
-        def interleave(engine, dst, src, lo, hi):
-            copier[engine](
-                out=dst[:, PACK * lo : PACK * hi].rearrange("p (c i t) -> p c t i", i=4, t=PACK),
-                in_=src.rearrange("p (t c) -> p t c", t=PACK)[:, :, lo:hi].rearrange("p t (c i) -> p c t i", i=4),
+            nc.scalar.activation(
+                x_rows[:, PJ * t : PJ * (t + 1)], diff[:], ACT.Abs, bias=zero_bias[:], scale=gain_cols[:, n : n + 1]
             )
 
-        def score_pass(b, mt):
-            rows = slice(P * mt, P * (mt + 1))
+        def interleave(copy, words, rows, lo, hi):
+            copy(
+                out=words[:, PACK * lo : PACK * hi].rearrange("p (c i t) -> p c t i", i=4, t=PACK),
+                in_=rows.rearrange("p (t c) -> p t c", t=PACK)[:, :, lo:hi].rearrange("p t (c i) -> p c t i", i=4),
+            )
+
+        def quantise_page(g, lo, hi):
+            quantise(page_codes[g][:, lo:hi], page_scales[g][:, lo:hi], page_words[:, PACK * lo : PACK * hi])
+
+        def quantise_x(g):
+            quantise(x_codes[g][:], x_scales[g][:], x_words[:])
+
+        def score_bank(mt):
+            return banks[(mt + 3) % BANKS]
+
+        def score_pass(g, mt):
+            cols = slice(P * mt, P * (mt + 1))
             nc.tensor.matmul_mx(
-                banks[(mt + 3) % 8][:], lhsT=page_codes[b][:, rows].bitcast(FP8X4), lhsT_scale=page_scales[b][:, rows],
-                rhs=x_codes[b][:].bitcast(FP8X4), rhs_scale=x_scales[b][:], start=(b == 0), stop=(b == PASSES - 1),
+                score_bank(mt)[:], lhsT=page_codes[g][:, cols].bitcast(FP8X4), lhsT_scale=page_scales[g][:, cols],
+                rhs=x_codes[g][:].bitcast(FP8X4), rhs_scale=x_scales[g][:], start=(g == 0), stop=(g == PASSES - 1),
             )
 
         def finish(mt):
-            bank, floor, result = banks[(mt + 3) % 8], base_cols[:, mt : mt + 1], briefs[mt]
-            if mt in BY_GPSIMD:
-                nc.scalar.copy(out=result[:], in_=bank[:])
-                nc.gpsimd.tensor_scalar(result[:], result[:], F32_MAX, floor, ALU.min, ALU.max)
-            else:
-                nc.vector.tensor_scalar(result[:], bank[:], floor, None, ALU.max)
-            nc.sync.dma_start(out=out[P * mt : P * (mt + 1), :], in_=result[:])
+            nc.vector.tensor_scalar(briefs[mt][:], score_bank(mt)[:], base_cols[:, mt : mt + 1], None, ALU.max)
+            nc.sync.dma_start(out=out[P * mt : P * (mt + 1), :], in_=briefs[mt][:])
+
 
         nc.gpsimd.memset(zero[:], 0.0)
         nc.scalar.activation(zero_bias[:], zero[:], ACT.Tanh)
-        nc.vector.memset(table_scales[:].rearrange("p a t -> p (a t)").bitcast(I32), 0)
-        nc.vector.memset(wa_scale[:].rearrange("p a t -> p (a t)").bitcast(I32), 0)
+        nc.vector.memset(table_scales[:].rearrange("p a c -> p (a c)").bitcast(I32), 0)
+        nc.vector.memset(wa_scale[:].rearrange("p a c -> p (a c)").bitcast(I32), 0)
         make_identity(nc, ident[:])
         nc.gpsimd.memset(base_rows[:], 0.0)
 
-        def load_table(a):
-            nc.sync.dma_start(out=table[a][:], in_=tab_words[a].rearrange("p t i -> p (t i)").bitcast(I32))
-
-        nc.sync.dma_start(lists[0][:], offs)
+        nc.sync.dma_start(table_list[:], offs)
         load_table(0)
-        load_scale_rows(nc.sync, table_scales, tab_scales)
+        load_scale_rows(table_scales, tab_scales)
         load_table(1)
-        load_scale_rows(nc.sync, wa_scale, wa_scales)
+        load_scale_rows(wa_scale, wa_scales)
         nc.sync.dma_start(out=wgs_rows[:], in_=wgs)
-        nc.sync.dma_start(out=wa_codes[:].bitcast(I32), in_=wa_words.rearrange("a p n -> p a n").bitcast(I32))
-        for unit in range(4):
-            load_weights(unit)
-        nc.sync.dma_start(lists[1][:], offs2)
+        nc.sync.dma_start(out=wa_codes[:].bitcast(I32), in_=wa_words.rearrange("a p c -> p a c").bitcast(I32))
+        for chunk in range(CHUNKS):
+            load_chunk(chunk)
+        nc.sync.dma_start(put_list[:], offs2)
         load_page(0)
-        nc.sync.dma_start(lists[2][:], offs3)
-        nc.sync.dma_start(out=gain_cols[:].rearrange("p (b t) -> p b t", t=PACK), in_=gain.rearrange("(b p t) -> p b t", p=P, t=PACK))
+        nc.sync.dma_start(fetch_list[:], offs3)
+        nc.sync.dma_start(
+            out=gain_cols[:].rearrange("p (g t) -> p g t", t=PACK), in_=gain.rearrange("(g p t) -> p g t", p=P, t=PACK)
+        )
         nc.sync.dma_start(out=base_rows[0:TILES, :], in_=base.rearrange("(n p) -> n p", p=P))
 
         for a in range(PASSES):
-            nc.vector.tensor_copy(v_scales[a][:], table_scales[:, a, :].indirect(lists[0][:]))
+            nc.vector.tensor_copy(v_scales[a][:], table_scales[:, a, :].indirect(table_list[:]))
         for a in range(PASSES):
-            nc.vector.tensor_copy(v_codes[a][:], table[a][:].bitcast(U32).indirect(lists[0][:]))
+            nc.vector.tensor_copy(v_codes[a][:], table[a][:].bitcast(U32).indirect(table_list[:]))
 
-        for part in range(4):
+        for part in range(PARTS):
             nc.tensor.transpose(banks[2][:, P * part : P * (part + 1)], wgs_rows[:, P * part : P * (part + 1)], ident[:])
         nc.scalar.copy(
-            out=wgs_turned[:].rearrange("j (c t q) -> j c t q", c=4, t=PACK), in_=banks[2][:].rearrange("j (c q t) -> j c t q", c=4, t=PACK)
+            out=wgs_turned[:].rearrange("j (part t q) -> j part t q", part=PARTS, t=PACK),
+            in_=banks[2][:].rearrange("j (part q t) -> j part t q", part=PARTS, t=PACK),
         )
-        for unit in range(4):
-            round_weights(unit, HEAD_ENG[unit])
-            quantise_weights(unit)
-        for step in LOADS.split():
-            {"w": load_weights, "p": load_page, "b": load_brief}[step[0]](int(step[1]))
-        products_bc(0)
-        add_gate(0)
-        for b in range(PASSES):
-            for part in range(4):
-                product_a_turned(b, part, banks[3 + (4 * b + part) % 5])
-            if b == 0:
+        for chunk in range(CHUNKS - 1):
+            (round_chunk if chunk < PASSES else round_chunk_on_two_engines)(chunk)
+            quantise_chunk(chunk, 0, SPAN)
+        round_chunk_on_two_engines(CHUNKS - 1)
+        for lo, hi in ((0, P), (P, 2 * P), (2 * P, SPAN)):
+            quantise_chunk(CHUNKS - 1, lo, hi)
+
+        for n, chunks in enumerate(LATER_CHUNKS):
+            for chunk in chunks:
+                load_chunk(chunk)
+            load_brief(n)
+            if n + 1 == PACK - 1:
+                load_page(PACK)
+            load_page(n + 1)
+        for n in range(PACK - 1, TILES):
+            if n + BRIEF_LAG < TILES:
+                load_page(n + BRIEF_LAG)
+            load_brief(n)
+
+        for g in range(PASSES):
+            for part in range(PARTS):
+                weigh_a_turned(g, part, banks[3 + (PARTS * g + part) % (BANKS - 3)])
+            if g == 0:
                 turn_weighted(0)
+        halves = ((0, S // 2), (S // 2, S))
+        product(0, 0, banks[0], 0, S)
+        for (lo, hi), bank in zip(halves, (banks[7], banks[1])):
+            product(0, 1, bank, lo, hi)
+            add_products(0, lo, hi)
         nc.gpsimd.tensor_scalar(not_negative[:], gain_cols[:], 0.0, None, ALU.is_ge)
         nc.gpsimd.tensor_scalar(sign_cols[:], not_negative[:], 2.0, -1.0, ALU.mult, ALU.add)
 
+
         last = TILES - 1
         for n in range(TILES):
-            put_columns(n)
+            for lo, hi in halves if n == 0 else ((0, S),):
+                put_columns(n, lo, hi)
             if n == PACK - 1:
-                for m in range(EARLY_PAGES):
-                    round_page(m)
+                round_page(0)
             if n < last:
-                products_bc(n + 1)
-                add_gate(n + 1)
+                for matrix in range(2):
+                    product(n + 1, matrix, banks[(n + 1 + matrix) % 2], 0, S)
+                add_products(n + 1, 0, S)
             if n < PACK:
                 turn_weighted(n + 1)
             if n >= 1:
                 round_x(n - 1)
-            if PACK <= n < LATE_FROM:
+            if PACK <= n < last - 1:
                 turn_weighted(n + 1)
             fetch_columns(n)
-            for unit in ROUND[n]:
-                round_weights(unit, "s")
-                quantise_weights(unit)
+            if n < len(LATER_CHUNKS):
+                for chunk in LATER_CHUNKS[n]:
+                    round_chunk(chunk)
+                    quantise_chunk(chunk, 0, SPAN)
             if n == PACK - 1:
-                for m in range(EARLY_PAGES, PACK - 1):
-                    round_page(m)
+                for earlier in range(1, PACK - 1):
+                    round_page(earlier)
             if n == PACK:
-                interleave(X0_ENG, x_grouped, x_rows[:], 0, PJ)
-                quantise(x_codes[0][:], x_scales[0][:], x_grouped[:])
+                interleave(nc.scalar.copy, x_words, x_rows[:], 0, PJ)
+                quantise_x(0)
                 round_page(PACK - 1)
-            if n in (PACK, PACK + 1):
-                for half in HALVES[n - PACK]:
-                    interleave("s", page_grouped, page_rows, 512 * half, 512 * (half + 1))
-                    quantise(page_codes[0][:, 512 * half : 512 * (half + 1)], page_scales[0][:, 512 * half : 512 * (half + 1)], page_grouped[:, 2048 * half : 2048 * (half + 1)])
-            if n == PACK + 2:
+            if n == PACK + 1:
+                for lo in (0, T2 // 2):
+                    interleave(nc.scalar.copy, page_words, page_rows, lo, lo + T2 // 2)
+                    quantise_page(0, lo, lo + T2 // 2)
+            if n == last - 1:
                 nc.tensor.transpose(banks[7][:, 0:P], base_rows[:], ident[:])
                 nc.scalar.copy(out=base_cols[:], in_=banks[7][:, 0:TILES])
-            if LATE_FROM <= n < last:
-                turn_weighted(n + 1)
-            if n == PACK + 2:
+                turn_weighted(last)
                 round_page(n - 2)
                 round_page(n - 1)
         round_page(last - 1)
         round_page(last)
         round_x(last)
+
+
         for mt in range(TILES):
             score_pass(0, mt)
-        interleave("v", x_grouped, x_rows[:], 0, PJ)
+        quarter = T2 // 4
+        interleave(nc.vector.tensor_copy, x_words, x_rows[:], 0, PJ)
         order = (2, 3, 0, 1)
-        for quarter in order:
-            interleave(TAIL_ENG[quarter], page_grouped, page_rows, 256 * quarter, 256 * (quarter + 1))
-        quantise(x_codes[1][:], x_scales[1][:], x_grouped[:])
-        for quarter in order:
-            cols = slice(256 * quarter, 256 * (quarter + 1))
-            quantise(page_codes[1][:, cols], page_scales[1][:, cols], page_grouped[:, 1024 * quarter : 1024 * (quarter + 1)])
-        for quarter in order:
-            for mt in (2 * quarter, 2 * quarter + 1):
-                score_pass(1, mt)
-        for quarter in order:
-            for mt in (2 * quarter, 2 * quarter + 1):
-                finish(mt)
+        for i in order:
+            copy = nc.vector.tensor_copy if i >= 2 else nc.scalar.copy
+            interleave(copy, page_words, page_rows, quarter * i, quarter * (i + 1))
+        quantise_x(1)
+        for i in order:
+            quantise_page(1, quarter * i, quarter * (i + 1))
+        out_tiles = [mt for i in order for mt in (2 * i, 2 * i + 1)]
+        for mt in out_tiles:
+            score_pass(1, mt)
+        for mt in out_tiles:
+            finish(mt)

from contextlib import ExitStack

import concourse.mybir as mybir
from concourse.masks import make_identity

K, T, S, H, T2, PJ = 1024, 2048, 512, 1024, 1024, 512
FLOPS = 2 * (3 * K * H * S + H * T2 * PJ)

F32 = mybir.dt.float32
BF16 = mybir.dt.bfloat16
I32 = mybir.dt.int32
U32 = mybir.dt.uint32
U16 = mybir.dt.uint16
U8 = mybir.dt.uint8
FP8X4 = mybir.dt.float8_e4m3fn_x4
FP4X4 = mybir.dt.float4_e2m1fn_x4
ALU = mybir.AluOpType
ACT = mybir.ActivationFunctionType

P = 128
PACK = 4
SPAN = P * PACK
PASSES = K // SPAN
TILES = PACK * PASSES
PARTS = S // P
BANKS = 8
CHUNKS = 2 * PASSES
SCALAR_GROUPS = 48
LATER_CHUNKS = ((4,), (5, 6), (7,))
BRIEF_LAG = 2


def tile_list_sector_clue_scores_kernel(
    tc, tab_words, tab_scales, offs, offs2, offs3, wa_words, wa_scales, wb, wc, wgs, page0, brief, gain, base, out
):
    nc = tc.nc
    with ExitStack() as ctx:
        sbuf = ctx.enter_context(tc.tile_pool(name="sbuf", bufs=1))
        psum = ctx.enter_context(tc.psum_pool(name="psum", bufs=1))

        def tiles(name, count, shape, dtype):
            return [sbuf.tile(shape, dtype, name="%s%d" % (name, i), align_bytes=64) for i in range(count)]

        table_list, put_list, fetch_list = [sbuf.tile([P, S // 16], U16, name="list%d" % i) for i in range(3)]
        table_scales = sbuf.tile([P, PASSES, T], U8, align_bytes=64)
        wa_scale = sbuf.tile([P, PASSES, H], U8, align_bytes=64)
        zero = sbuf.tile([P, 1], F32, align_bytes=64)
        zero_bias = sbuf.tile([P, 1], F32, align_bytes=64)
        banks = [psum.tile([P, 512], F32, name="bank%d" % i) for i in range(BANKS)]
        table = tiles("table", PASSES, [P, T], I32)
        v_codes = tiles("v_codes", PASSES, [P, S], U32)
        v_scales = tiles("v_scales", PASSES, [P, S], U8)
        wa_codes = sbuf.tile([P, PASSES, 2 * H], U8, align_bytes=64)
        wgs_rows = sbuf.tile([P, S], F32, align_bytes=64)
        wgs_turned = sbuf.tile([P, S], F32, align_bytes=64)
        weighted_turned = tiles("weighted_turned", PASSES * PARTS, [P, SPAN], F32)
        weighted_pair = tiles("weighted_pair", 2, [P, S], F32)
        raw = tiles("raw", CHUNKS, [P, PACK * SPAN], F32)
        rounded = tiles("rounded", CHUNKS, [P, PACK * SPAN], BF16)
        w_codes = tiles("w_codes", PASSES * CHUNKS, [P, SPAN], U32)
        w_scales = tiles("w_scales", PASSES * CHUNKS, [P, SPAN], U8)
        page = tiles("page", TILES, [P, T2], F32)
        briefs = tiles("briefs", TILES, [P, PJ], F32)
        tanh_b = tiles("tanh_b", 2, [P, S], F32)
        abs_c = tiles("abs_c", 2, [P, S], F32)
        sums = tiles("sums", 3, [P, S], F32)
        diff = sbuf.tile([P, PJ], F32, align_bytes=64)
        page_rows = raw[CHUNKS - 1][:].bitcast(BF16)
        page_words = sbuf.tile([P, PACK * T2], BF16, align_bytes=64)
        x_rows = sbuf.tile([P, PACK * PJ], BF16, align_bytes=64)
        x_words = sbuf.tile([P, PACK * PJ], BF16, align_bytes=64)
        page_codes = tiles("page_codes", PASSES, [P, T2], U32)
        page_scales = tiles("page_scales", PASSES, [P, T2], U8)
        x_codes = w_codes[0:PASSES]
        x_scales = w_scales[0:PASSES]
        ident = sbuf.tile([P, P], F32, align_bytes=64)
        base_rows = sbuf.tile([P, P], F32, align_bytes=64)
        base_cols = sbuf.tile([P, TILES], F32, align_bytes=64)
        gain_cols = sbuf.tile([P, TILES], F32, align_bytes=64)
        not_negative = sbuf.tile([P, TILES], F32, align_bytes=64)
        sign_cols = sbuf.tile([P, TILES], F32, align_bytes=64)


        def load_table(a):
            nc.sync.dma_start(out=table[a][:], in_=tab_words[a].rearrange("p c i -> p (c i)").bitcast(I32))

        def load_scale_rows(dst, src):
            for quad in range(4):
                nc.sync.dma_start(
                    out=dst[32 * quad : 32 * quad + 4, :, :].bitcast(I32),
                    in_=src[:, 4 * quad : 4 * quad + 4, :].rearrange("a s c -> s a c").bitcast(I32),
                )

        def load_chunk(chunk):
            g, matrix, a = chunk // CHUNKS, chunk % CHUNKS // PASSES, chunk % PASSES
            src = (wb, wc)[matrix][SPAN * a : SPAN * (a + 1), SPAN * g : SPAN * (g + 1)]
            nc.sync.dma_start(
                out=raw[chunk % CHUNKS][:].rearrange("p (i c) -> p i c", i=PACK), in_=src.rearrange("(p i) c -> p i c", i=PACK)
            )

        def tile_rows(src, n):
            return src.rearrange("(g p t) c -> g t p c", g=PASSES, t=PACK)[n // PACK, n % PACK]

        def load_page(n):
            nc.sync.dma_start(out=page[n][:], in_=tile_rows(page0, n))

        def load_brief(n):
            nc.sync.dma_start(out=briefs[n][:], in_=tile_rows(brief, n))


        def quantise(codes, scales, values):
            nc.vector.quantize_mx(out=codes.bitcast(FP8X4), scales=scales, in_=values)

        def chunk_views(chunk):
            dst = rounded[chunk % CHUNKS][:].rearrange("p (t q i) -> p q i t", t=PACK, i=PACK)
            src = raw[chunk % CHUNKS][:].rearrange("p (i q t) -> p q i t", t=PACK, i=PACK)
            return dst, src

        def round_chunk(chunk):
            dst, src = chunk_views(chunk)
            nc.scalar.copy(out=dst, in_=src)

        def round_chunk_on_two_engines(chunk):
            dst, src = chunk_views(chunk)
            nc.scalar.copy(out=dst[:, :SCALAR_GROUPS], in_=src[:, :SCALAR_GROUPS])
            nc.vector.tensor_copy(out=dst[:, SCALAR_GROUPS:], in_=src[:, SCALAR_GROUPS:])

        def quantise_chunk(chunk, lo, hi):
            quantise(w_codes[chunk][:, lo:hi], w_scales[chunk][:, lo:hi], rounded[chunk % CHUNKS][:, PACK * lo : PACK * hi])

        def product(n, matrix, bank, lo, hi):
            cols = slice(P * (n % PACK), P * (n % PACK + 1))
            dst, func = ((tanh_b, ACT.Tanh), (abs_c, ACT.Abs))[matrix]
            for a in range(PASSES):
                chunk = CHUNKS * (n // PACK) + PASSES * matrix + a
                nc.tensor.matmul_mx(
                    bank[:, lo:hi], lhsT=w_codes[chunk][:, cols].bitcast(FP8X4), lhsT_scale=w_scales[chunk][:, cols],
                    rhs=v_codes[a][:, lo:hi].bitcast(FP8X4), rhs_scale=v_scales[a][:, lo:hi],
                    start=(a == 0), stop=(a == PASSES - 1),
                )
            nc.scalar.activation(dst[n % 2][:, lo:hi], bank[:, lo:hi], func, bias=zero_bias[:])

        def add_products(n, lo, hi):
            nc.vector.tensor_tensor(sums[n % 3][:, lo:hi], tanh_b[n % 2][:, lo:hi], abs_c[n % 2][:, lo:hi], ALU.add)

        def weigh_a_turned(g, part, bank):
            entries = slice(P * part, P * (part + 1))
            for a in range(PASSES):
                nc.tensor.matmul_mx(
                    bank[:], lhsT=v_codes[a][:, entries].bitcast(FP8X4), lhsT_scale=v_scales[a][:, entries],
                    rhs=wa_codes[:, a, 2 * SPAN * g : 2 * SPAN * (g + 1)].bitcast(FP4X4),
                    rhs_scale=wa_scale[:, a, SPAN * g : SPAN * (g + 1)],
                    start=(a == 0), stop=(a == PASSES - 1),
                )
            factors = wgs_turned[:, entries].rearrange("j (t q) -> j t q", t=PACK).unsqueeze(2).to_broadcast([P, PACK, 4, 32])
            nc.vector.tensor_tensor(
                weighted_turned[PARTS * g + part][:].rearrange("j (t u q) -> j t u q", t=PACK, u=4),
                bank[:].rearrange("j (u q t) -> j t u q", t=PACK, u=4), factors, ALU.mult,
            )

        def weighted(n):
            if n % PACK == 0:
                return rounded[CHUNKS - 1 if n else 1][:, 0 : 2 * S].bitcast(F32)
            return weighted_pair[n % 2][:]

        def turn_weighted(n):
            bank = banks[(n + 1) % 2 if 0 < n < PACK else 2]
            for part in range(PARTS):
                src = weighted_turned[PARTS * (n // PACK) + part]
                nc.tensor.transpose(bank[:, P * part : P * (part + 1)], src[:, P * (n % PACK) : P * (n % PACK + 1)], ident[:])
            nc.scalar.copy(out=weighted(n), in_=bank[:])

        def put_columns(n, lo, hi):
            offsets = put_list[:, lo // 16 : hi // 16]
            nc.vector.tensor_tensor(page[n][:].indirect(offsets), sums[n % 3][:, lo:hi], weighted(n)[:, lo:hi], ALU.mult)


        def fetch_columns(n):
            nc.vector.tensor_tensor(diff[:], page[n][:].indirect(fetch_list[:]), briefs[n][:], ALU.subtract)

        def round_page(n):
            t = n % PACK
            nc.scalar.activation(page_rows[:, T2 * t : T2 * (t + 1)], page[n][:], ACT.Copy, scale=sign_cols[:, n : n + 1])

        def round_x(n):
            t = n % PACK
            nc.scalar.activation(
                x_rows[:, PJ * t : PJ * (t + 1)], diff[:], ACT.Abs, bias=zero_bias[:], scale=gain_cols[:, n : n + 1]
            )

        def interleave(copy, words, rows, lo, hi):
            copy(
                out=words[:, PACK * lo : PACK * hi].rearrange("p (c i t) -> p c t i", i=4, t=PACK),
                in_=rows.rearrange("p (t c) -> p t c", t=PACK)[:, :, lo:hi].rearrange("p t (c i) -> p c t i", i=4),
            )

        def quantise_page(g, lo, hi):
            quantise(page_codes[g][:, lo:hi], page_scales[g][:, lo:hi], page_words[:, PACK * lo : PACK * hi])

        def quantise_x(g):
            quantise(x_codes[g][:], x_scales[g][:], x_words[:])

        def score_bank(mt):
            return banks[(mt + 3) % BANKS]

        def score_pass(g, mt):
            cols = slice(P * mt, P * (mt + 1))
            nc.tensor.matmul_mx(
                score_bank(mt)[:], lhsT=page_codes[g][:, cols].bitcast(FP8X4), lhsT_scale=page_scales[g][:, cols],
                rhs=x_codes[g][:].bitcast(FP8X4), rhs_scale=x_scales[g][:], start=(g == 0), stop=(g == PASSES - 1),
            )

        def finish(mt):
            nc.vector.tensor_scalar(briefs[mt][:], score_bank(mt)[:], base_cols[:, mt : mt + 1], None, ALU.max)
            nc.sync.dma_start(out=out[P * mt : P * (mt + 1), :], in_=briefs[mt][:])


        nc.gpsimd.memset(zero[:], 0.0)
        nc.scalar.activation(zero_bias[:], zero[:], ACT.Tanh)
        nc.vector.memset(table_scales[:].rearrange("p a c -> p (a c)").bitcast(I32), 0)
        nc.vector.memset(wa_scale[:].rearrange("p a c -> p (a c)").bitcast(I32), 0)
        make_identity(nc, ident[:])
        nc.gpsimd.memset(base_rows[:], 0.0)

        nc.sync.dma_start(table_list[:], offs)
        load_table(0)
        load_scale_rows(table_scales, tab_scales)
        load_table(1)
        load_scale_rows(wa_scale, wa_scales)
        nc.sync.dma_start(out=wgs_rows[:], in_=wgs)
        nc.sync.dma_start(out=wa_codes[:].bitcast(I32), in_=wa_words.rearrange("a p c -> p a c").bitcast(I32))
        for chunk in range(CHUNKS):
            load_chunk(chunk)
        nc.sync.dma_start(put_list[:], offs2)
        load_page(0)
        nc.sync.dma_start(fetch_list[:], offs3)
        nc.sync.dma_start(
            out=gain_cols[:].rearrange("p (g t) -> p g t", t=PACK), in_=gain.rearrange("(g p t) -> p g t", p=P, t=PACK)
        )
        nc.sync.dma_start(out=base_rows[0:TILES, :], in_=base.rearrange("(n p) -> n p", p=P))

        for a in range(PASSES):
            nc.vector.tensor_copy(v_scales[a][:], table_scales[:, a, :].indirect(table_list[:]))
        for a in range(PASSES):
            nc.vector.tensor_copy(v_codes[a][:], table[a][:].bitcast(U32).indirect(table_list[:]))

        for part in range(PARTS):
            nc.tensor.transpose(banks[2][:, P * part : P * (part + 1)], wgs_rows[:, P * part : P * (part + 1)], ident[:])
        nc.scalar.copy(
            out=wgs_turned[:].rearrange("j (part t q) -> j part t q", part=PARTS, t=PACK),
            in_=banks[2][:].rearrange("j (part q t) -> j part t q", part=PARTS, t=PACK),
        )
        for chunk in range(CHUNKS - 1):
            (round_chunk if chunk < PASSES else round_chunk_on_two_engines)(chunk)
            quantise_chunk(chunk, 0, SPAN)
        round_chunk_on_two_engines(CHUNKS - 1)
        for lo, hi in ((0, P), (P, 2 * P), (2 * P, SPAN)):
            quantise_chunk(CHUNKS - 1, lo, hi)

        for n, chunks in enumerate(LATER_CHUNKS):
            for chunk in chunks:
                load_chunk(chunk)
            load_brief(n)
            if n + 1 == PACK - 1:
                load_page(PACK)
            load_page(n + 1)
        for n in range(PACK - 1, TILES):
            if n + BRIEF_LAG < TILES:
                load_page(n + BRIEF_LAG)
            load_brief(n)

        for g in range(PASSES):
            for part in range(PARTS):
                weigh_a_turned(g, part, banks[3 + (PARTS * g + part) % (BANKS - 3)])
            if g == 0:
                turn_weighted(0)
        halves = ((0, S // 2), (S // 2, S))
        product(0, 0, banks[0], 0, S)
        for (lo, hi), bank in zip(halves, (banks[7], banks[1])):
            product(0, 1, bank, lo, hi)
            add_products(0, lo, hi)
        nc.gpsimd.tensor_scalar(not_negative[:], gain_cols[:], 0.0, None, ALU.is_ge)
        nc.gpsimd.tensor_scalar(sign_cols[:], not_negative[:], 2.0, -1.0, ALU.mult, ALU.add)


        last = TILES - 1
        for n in range(TILES):
            for lo, hi in halves if n == 0 else ((0, S),):
                put_columns(n, lo, hi)
            if n == PACK - 1:
                round_page(0)
            if n < last:
                for matrix in range(2):
                    product(n + 1, matrix, banks[(n + 1 + matrix) % 2], 0, S)
                add_products(n + 1, 0, S)
            if n < PACK:
                turn_weighted(n + 1)
            if n >= 1:
                round_x(n - 1)
            if PACK <= n < last - 1:
                turn_weighted(n + 1)
            fetch_columns(n)
            if n < len(LATER_CHUNKS):
                for chunk in LATER_CHUNKS[n]:
                    round_chunk(chunk)
                    quantise_chunk(chunk, 0, SPAN)
            if n == PACK - 1:
                for earlier in range(1, PACK - 1):
                    round_page(earlier)
            if n == PACK:
                interleave(nc.scalar.copy, x_words, x_rows[:], 0, PJ)
                quantise_x(0)
                round_page(PACK - 1)
            if n == PACK + 1:
                for lo in (0, T2 // 2):
                    interleave(nc.scalar.copy, page_words, page_rows, lo, lo + T2 // 2)
                    quantise_page(0, lo, lo + T2 // 2)
            if n == last - 1:
                nc.tensor.transpose(banks[7][:, 0:P], base_rows[:], ident[:])
                nc.scalar.copy(out=base_cols[:], in_=banks[7][:, 0:TILES])
                turn_weighted(last)
                round_page(n - 2)
                round_page(n - 1)
        round_page(last - 1)
        round_page(last)
        round_x(last)


        for mt in range(TILES):
            score_pass(0, mt)
        quarter = T2 // 4
        interleave(nc.vector.tensor_copy, x_words, x_rows[:], 0, PJ)
        order = (2, 3, 0, 1)
        for i in order:
            copy = nc.vector.tensor_copy if i >= 2 else nc.scalar.copy
            interleave(copy, page_words, page_rows, quarter * i, quarter * (i + 1))
        quantise_x(1)
        for i in order:
            quantise_page(1, quarter * i, quarter * (i + 1))
        out_tiles = [mt for i in order for mt in (2 * i, 2 * i + 1)]
        for mt in out_tiles:
            score_pass(1, mt)
        for mt in out_tiles:
            finish(mt)
